import numpy as np
import ml_dtypes


def mxq(x, axis, fmt="e4m3"):
    dtype, down = {"e4m3": (ml_dtypes.float8_e4m3fn, 7), "e5m2": (ml_dtypes.float8_e5m2, 14)}[fmt]
    v = np.moveaxis(np.asarray(x, np.float32).astype(ml_dtypes.bfloat16).astype(np.float64), axis, -1)
    blocks = v.reshape(v.shape[:-1] + (-1, 32))
    amax = np.abs(blocks).max(-1, keepdims=True)
    byte = np.maximum(np.where(amax > 0, np.frexp(amax)[1] - 1 + 127, 0) - down, 1)
    scale = np.exp2(byte - 127.0)
    codes = (blocks / scale).astype(np.float32).astype(dtype).astype(np.float64)
    return np.moveaxis((codes * scale).reshape(v.shape), -1, axis)


WIDE = False


def mx_kscale(k):
    if not WIDE:
        return np.ones(k)
    levels = np.array([10, -10, 5, -5, 0])
    if k % 512:
        return np.exp2(np.random.permutation(np.resize(levels, k // 32))).repeat(32)
    a = np.empty((k // 512, 16))
    for p in range(k // 512):
        a[p, :8] = np.random.permutation(np.resize(levels, 8))
        for g in range(8):
            far = levels[np.abs(levels - a[p, g]) >= 10]
            a[p, g + 8] = far[np.random.randint(len(far))]
    return np.exp2(a.ravel()).repeat(32)


BF16 = ml_dtypes.bfloat16


def bf(x):
    return np.asarray(x, np.float32).astype(BF16)


def f64(x):
    return np.asarray(x).astype(np.float64)


E2M1 = np.array([0.0, 0.5, 1.0, 1.5, 2.0, 3.0, 4.0, 6.0, -0.0, -0.5, -1.0, -1.5, -2.0, -3.0, -4.0, -6.0])


def pack_weight(w, fmt):
    k, n = w.shape
    w = f64(bf(w)).reshape(k // 32, 32, n)
    amax = np.abs(w).max(1)
    if fmt == "e4m3":
        byte = np.frexp(amax)[1] - 1 + 127 - 7
    else:
        mant, ex = np.frexp(amax / 6.0)
        byte = np.where(mant > 0.5, ex, ex - 1) + 127
    byte = np.clip(np.where(amax > 0, byte, 1), 1, 254)
    scaled = (w * np.exp2(127.0 - byte)[:, None, :]).reshape(k, n).astype(np.float32)
    by_word = np.ascontiguousarray(scaled.reshape(k // 512, 128, 4, n).transpose(0, 1, 3, 2))
    if fmt == "e4m3":
        words = by_word.astype(ml_dtypes.float8_e4m3fn).view(np.uint8)
    else:
        c = by_word.astype(ml_dtypes.float4_e2m1fn).view(np.uint8) & 0xF
        words = c[..., 0::2] | (c[..., 1::2] << 4)
    return np.ascontiguousarray(words), np.ascontiguousarray(byte.astype(np.uint8).reshape(k // 512, 16, n))


def unpack_weight(words, scales, fmt):
    g, p, n, _ = words.shape
    if fmt == "e4m3":
        vals = np.ascontiguousarray(words).view(ml_dtypes.float8_e4m3fn).astype(np.float64)
    else:
        nib = np.empty((g, p, n, 4), np.uint8)
        nib[..., 0::2] = words & 0xF
        nib[..., 1::2] = words >> 4
        vals = E2M1[nib]
    vals = vals * np.repeat(np.exp2(scales.astype(np.float64) - 127.0), 8, axis=1)[..., None]
    return vals.transpose(0, 1, 3, 2).reshape(g * 512, n)
def pack4(w):
    words, scales = pack_weight(w, "e2m1")
    return words.reshape(words.shape[0], 128, -1), scales


def unpack4(words, scales):
    return unpack_weight(words.reshape(words.shape[0], 128, -1, 2), scales, "e2m1")


M, K, F, L, D = 1024, 512, 1024, 6, 256
P = L * D
MAX_FREQ = 1000.0


def draw0():
    s, t, u = mx_kscale(K), mx_kscale(F), mx_kscale(M)
    level = np.random.random(M)
    phase = level[:, None] * MAX_FREQ ** np.linspace(0.0, 1.0, K // 2)
    emb = np.concatenate([np.cos(phase), np.sin(phase)], axis=1)
    w1 = np.random.standard_normal((K, F)) * 2.0 / np.sqrt(K)
    table = np.random.standard_normal((F, P)) / np.sqrt(F)
    table_words, table_scales = pack4(table / t[:, None])
    return {"emb": bf(emb * s),
            "w1": bf(w1 / s[:, None]),
            "gain": bf((1 + 0.1 * np.random.standard_normal(F)) * t),
            "table_words": table_words,
            "table_scales": table_scales,
            "level_weight": bf(np.exp(0.5 * np.random.standard_normal(M)) / np.sqrt(M) * u),
            "teacher": bf(np.random.standard_normal((M, P)) / u[:, None])}


def core(emb, w1, gain, table_words, table_scales, level_weight, teacher):
    z = mxq(f64(emb), 1, "e4m3") @ mxq(f64(w1), 0, "e4m3")
    h = z / (1 + np.exp(-z))
    a = h * f64(gain)
    b = h * f64(level_weight)[:, None]
    bias = mxq(a, 1, "e4m3") @ unpack4(table_words, table_scales)
    moments = mxq(b, 0, "e4m3").T @ mxq(f64(teacher), 0, "e4m3")
    return bias, moments


def e4m3fn_bytes(y):
    return np.clip(np.asarray(y, np.float64), -448.0, 448.0).astype(np.float32).astype(ml_dtypes.float8_e4m3fn).view(np.uint8)


def e4m3fn_values(b):
    return np.asarray(b, np.uint8).view(ml_dtypes.float8_e4m3fn).astype(np.float64)


def setup_inputs():
    d = draw0()
    x0 = np.asarray(d['teacher']).astype(np.float64)
    s = (np.max(np.abs(x0), axis=(1,), keepdims=True) / 448.0).astype(np.float32)
    out = {}
    for k, v in d.items():
        if k == 'teacher':
            out['teacher_bytes'] = e4m3fn_bytes(x0 / s.astype(np.float64))
            out['teacher_scale'] = s
        else:
            out[k] = v
    return out


def reference(emb, w1, gain, table_words, table_scales, level_weight, teacher_bytes, teacher_scale):
    return core(emb, w1, gain, table_words, table_scales, level_weight, e4m3fn_values(teacher_bytes) * teacher_scale.astype(np.float64))

@@ -1,0 +1,367 @@
+from contextlib import ExitStack
+
+import concourse.mybir as mybir
+from concourse.masks import make_identity
+
+M, K, F, PCOLS = 1024, 512, 1024, 1536
+FLOPS = 2 * M * K * F + 4 * M * F * PCOLS
+
+F32 = mybir.dt.float32
+BF16 = mybir.dt.bfloat16
+I32 = mybir.dt.int32
+U32 = mybir.dt.uint32
+U8 = mybir.dt.uint8
+FP8 = mybir.dt.float8_e4m3fn
+FP8X4 = mybir.dt.float8_e4m3fn_x4
+FP4X4 = mybir.dt.float4_e2m1fn_x4
+ACT = mybir.ActivationFunctionType
+MULT = mybir.AluOpType.mult
+
+P = 128
+NB = 512
+NCH = PCOLS // NB
+
+
+def tile_timestep_bias_table_calibration_s8_kernel(
+    tc, emb, w1, gain, table_words, table_scales, level_weight, teacher_bytes, teacher_scale, out_0, out_1
+):
+    nc = tc.nc
+    with ExitStack() as ctx:
+        keep = ctx.enter_context(tc.tile_pool(name="keep", bufs=1))
+        work = ctx.enter_context(tc.tile_pool(name="work", bufs=2))
+        psum = ctx.enter_context(tc.psum_pool(name="psum", bufs=2))
+        ctx.enter_context(tc.manual_schedule())
+
+        emb_raw = [keep.tile([P, 4, K], BF16, name="emb_raw%d" % g, align_bytes=64) for g in range(2)]
+        w1_raw = [keep.tile([P, 4, NB], BF16, name="w1_raw%d" % g, align_bytes=64) for g in range(2)]
+        w1_g = [keep.tile([P, NB, 4], BF16, name="w1_g%d" % g, align_bytes=64) for g in range(2)]
+        w1_c = [keep.tile([P, NB], U32, name="w1_c%d" % g, align_bytes=64) for g in range(2)]
+        w1_s = [keep.tile([P, NB], U8, name="w1_s%d" % g, align_bytes=64) for g in range(2)]
+        emb_g = [keep.tile([P, 4, P, 4], BF16, name="emb_g%d" % g, align_bytes=64) for g in range(2)]
+        emb_c = [keep.tile([P, 4 * P], U32, name="emb_c%d" % g, align_bytes=64) for g in range(2)]
+        emb_s = [keep.tile([P, 4 * P], U8, name="emb_s%d" % g, align_bytes=64) for g in range(2)]
+        h_sb = [[keep.tile([P, 4, NB], F32, name="h%d%d" % (g, fg), align_bytes=64) for fg in range(2)] for g in range(2)]
+        b_c = [[keep.tile([P, NB], U32, name="b_c%d%d" % (g, fg), align_bytes=64) for fg in range(2)] for g in range(2)]
+        b_s = [[keep.tile([P, NB], U8, name="b_s%d%d" % (g, fg), align_bytes=64) for fg in range(2)] for g in range(2)]
+        t_words = keep.tile([P, 2, 2 * PCOLS], U8, name="t_words", align_bytes=64)
+        t_scales = keep.tile([P, 2, PCOLS], U8, name="t_scales", align_bytes=64)
+        te_bytes = [keep.tile([P, 4, PCOLS], U8, name="te_bytes%d" % g, align_bytes=64) for g in range(2)]
+        te_c = [[keep.tile([P, NB], U32, name="te_c%d%d" % (g, c), align_bytes=64) for c in range(NCH)] for g in range(2)]
+        te_s = [[keep.tile([P, NB], U8, name="te_s%d%d" % (g, c), align_bytes=64) for c in range(NCH)] for g in range(2)]
+        gain_t = keep.tile([P, 2, 4], BF16, name="gain_t", align_bytes=64)
+        lw_t = keep.tile([P, 2, 4], BF16, name="lw_t", align_bytes=64)
+        ts_t = keep.tile([P, 2, 4], F32, name="ts_t", align_bytes=64)
+        ident = keep.tile([P, P], F32, name="ident", align_bytes=64)
+        warm = keep.tile([P, 8], F32, name="warm", align_bytes=64)
+
+        emb_v = emb.rearrange("(g p t) k -> g p t k", p=P, t=4)
+        w1_v = w1.rearrange("(p j) f -> p j f", j=4)
+        te_v = teacher_bytes.rearrange("(g p t) c -> g p t c", p=P, t=4)
+        out0_v = out_0.rearrange("(g p t) c -> g t p c", p=P, t=4)
+        out1_v = out_1.rearrange("(g p t) c -> g t p c", p=P, t=4)
+
+        nc.gpsimd.memset(warm[:], 0.0)
+        nc.scalar.dma_start(out=gain_t[:], in_=gain.rearrange("(g p t) -> p g t", p=P, t=4))
+        nc.scalar.dma_start(out=lw_t[:], in_=level_weight.rearrange("(g p t) -> p g t", p=P, t=4))
+        nc.scalar.dma_start(out=ts_t[:], in_=teacher_scale.rearrange("(g p t) o -> p g (t o)", p=P, t=4))
+        nc.scalar.activation(out=warm[:, 0:1], in_=warm[:, 1:2], func=ACT.Silu)
+        make_identity(nc, ident[:])
+        nc.vector.memset(t_scales[:].rearrange("p g n -> p (g n)").bitcast(I32), 0)
+
+        def load_teacher(g, c0, c1):
+            cols = slice(c0 * NB, c1 * NB)
+            nc.sync.dma_start(out=te_bytes[g][:, :, cols], in_=te_v[g][:, :, cols])
+
+        nc.sync.dma_start(out=emb_raw[0][:, 0:2, :], in_=emb_v[0][:, 0:2, :])
+        nc.sync.dma_start(out=w1_raw[0][:], in_=w1_v[:, :, 0:NB])
+        nc.sync.dma_start(out=emb_raw[0][:, 2:4, :], in_=emb_v[0][:, 2:4, :])
+        nc.sync.dma_start(out=w1_raw[1][:], in_=w1_v[:, :, NB:F])
+        load_teacher(0, 0, 1)
+        for g in range(2):
+            nc.sync.dma_start(out=t_words[:, g, :].bitcast(I32), in_=table_words[g].bitcast(I32))
+        for q in range(4):
+            nc.sync.dma_start(
+                out=t_scales[32 * q : 32 * q + 4, :, :].bitcast(I32),
+                in_=table_scales[:, 4 * q : 4 * q + 4, :].rearrange("g q n -> q g n").bitcast(I32),
+            )
+        nc.sync.dma_start(out=emb_raw[1][:], in_=emb_v[1])
+        load_teacher(1, 0, 1)
+        load_teacher(0, 1, 3)
+        load_teacher(1, 1, 3)
+
+        def bank(tag):
+            return psum.tile([P, NB], F32, name="ps_" + tag, tag=tag, bufs=4 if tag == "o" else 2)
+
+        def emb_transpose(g, half, tag):
+            xt = bank(tag)
+            for tt in range(2):
+                words = emb_raw[g][:, 2 * half + tt, :].bitcast(F32)
+                for u in range(2):
+                    at = (2 * tt + u) * P
+                    nc.tensor.transpose(xt[:, at : at + P], words[:, u : K // 2 : 2], ident[:])
+            return xt
+
+        def emb_evac(g, half, xt, copy=nc.scalar.copy):
+            copy(
+                out=emb_g[g][:, 2 * half : 2 * half + 2, :, :].rearrange("p t r k -> p t (r k)").bitcast(F32).rearrange("p t (r u) -> p t r u", u=2),
+                in_=xt[:].rearrange("p (t u r) -> p t r u", t=2, u=2),
+            )
+
+        def emb_quant(g, half):
+            cols = slice(2 * half * P, (2 * half + 2) * P)
+            nc.vector.quantize_mx(
+                out=emb_c[g][:, cols].bitcast(FP8X4),
+                scales=emb_s[g][:, cols],
+                in_=emb_g[g][:, 2 * half : 2 * half + 2, :, :].rearrange("p t r k -> p (t r k)"),
+            )
+
+        def w1_inter(eng, fg, c0, c1):
+            o = w1_g[fg][:, c0:c1, :]
+            i = w1_raw[fg][:, :, c0:c1].rearrange("p j w -> p w j")
+            if eng is nc.vector:
+                nc.vector.tensor_copy(out=o, in_=i)
+            else:
+                nc.scalar.copy(out=o, in_=i)
+
+        def w1_quant(fg):
+            nc.vector.quantize_mx(
+                out=w1_c[fg][:].bitcast(FP8X4), scales=w1_s[fg][:], in_=w1_g[fg][:].rearrange("p w j -> p (w j)")
+            )
+
+        zb = {}
+        tb = {}
+        ag = {}
+        ac = {}
+        ob = {}
+        wd = {}
+        tg = {}
+
+        def z_mm(i, fg):
+            g, t = divmod(i, 4)
+            z = bank("z")
+            nc.tensor.matmul_mx(
+                out=z[:],
+                lhsT=emb_c[g][:, t * P : (t + 1) * P].bitcast(FP8X4),
+                lhsT_scale=emb_s[g][:, t * P : (t + 1) * P],
+                rhs=w1_c[fg][:].bitcast(FP8X4),
+                rhs_scale=w1_s[fg][:],
+                start=True,
+                stop=True,
+            )
+            zb[i, fg] = z
+
+        def silu(i, fg):
+            g, t = divmod(i, 4)
+            nc.scalar.activation(
+                out=h_sb[g][fg][:, t, :].rearrange("p (t m) -> p t m", t=4),
+                in_=zb.pop((i, fg))[:].rearrange("p (m t) -> p t m", t=4),
+                func=ACT.Silu,
+            )
+
+        def h_transpose(i, fg):
+            g, t = divmod(i, 4)
+            x = bank("t")
+            for tf in range(4):
+                nc.tensor.transpose(x[:, tf * P : (tf + 1) * P], h_sb[g][fg][:, t, tf * P : (tf + 1) * P], ident[:])
+            tb[i, fg] = x
+
+        def a_mult(i, fg):
+            if i not in ag:
+                ag[i] = work.tile([P, 2, P, 4], BF16, name="a_g", tag="a_g", bufs=3, align_bytes=64)
+            nc.vector.tensor_tensor(
+                out=ag[i][:, fg, :, :],
+                in0=tb.pop((i, fg))[:].rearrange("p (t m) -> p m t", t=4),
+                in1=gain_t[:, fg, :].unsqueeze(1).to_broadcast([P, P, 4]),
+                op=MULT,
+            )
+
+        def a_quant(i):
+            c = work.tile([P, 2 * P], U32, name="a_c", tag="a_c", bufs=3, align_bytes=64)
+            s = work.tile([P, 2 * P], U8, name="a_s", tag="a_s", bufs=3, align_bytes=64)
+            nc.vector.quantize_mx(out=c[:].bitcast(FP8X4), scales=s[:], in_=ag.pop(i)[:].rearrange("p g m t -> p (g m t)"))
+            ac[i] = (c, s)
+
+        def bias_mm(i):
+            c, s = ac.pop(i)
+            for n in range(NCH):
+                o = bank("o")
+                for fg in range(2):
+                    nc.tensor.matmul_mx(
+                        out=o[:],
+                        lhsT=c[:, fg * P : (fg + 1) * P].bitcast(FP8X4),
+                        lhsT_scale=s[:, fg * P : (fg + 1) * P],
+                        rhs=t_words[:, fg, 2 * NB * n : 2 * NB * (n + 1)].bitcast(FP4X4),
+                        rhs_scale=t_scales[:, fg, NB * n : NB * (n + 1)],
+                        start=(fg == 0),
+                        stop=(fg == 1),
+                    )
+                ob[i, n] = o
+
+        def bias_out(i):
+            g, t = divmod(i, 4)
+            r = work.tile([P, PCOLS], F32, name="r0", tag="r0", bufs=4, align_bytes=64)
+            for n in range(NCH):
+                nc.scalar.copy(out=r[:, n * NB : (n + 1) * NB], in_=ob.pop((i, n))[:])
+            nc.sync.dma_start(out=out0_v[g, t], in_=r[:])
+
+        bgs = {}
+
+        def b_mult(g, fg):
+            bt = work.tile([P, NB, 4], BF16, name="b_g", tag="b_g", bufs=2, align_bytes=64)
+            nc.vector.tensor_tensor(
+                out=bt[:],
+                in0=h_sb[g][fg][:].rearrange("p t f -> p f t"),
+                in1=lw_t[:, g, :].unsqueeze(1).to_broadcast([P, NB, 4]),
+                op=MULT,
+            )
+            bgs[g, fg] = bt
+
+        def b_quant(g, fg):
+            nc.vector.quantize_mx(
+                out=b_c[g][fg][:].bitcast(FP8X4), scales=b_s[g][fg][:], in_=bgs.pop((g, fg))[:].rearrange("p f t -> p (f t)")
+            )
+
+        def te_widen(eng, g, c, t):
+            if t == 0:
+                wd[g, c] = work.tile([P, 4, NB], BF16, name="wide", tag="wide", bufs=3, align_bytes=64)
+            o = wd[g, c][:, t, :]
+            i = te_bytes[g][:, t, c * NB : (c + 1) * NB].bitcast(FP8)
+            if eng is nc.vector:
+                nc.vector.tensor_scalar(out=o, in0=i, scalar1=ts_t[:, g, t : t + 1], scalar2=None, op0=MULT)
+            else:
+                nc.scalar.activation(out=o, in_=i, func=ACT.Copy, scale=ts_t[:, g, t : t + 1])
+
+        def te_inter(g, c):
+            x = work.tile([P, NB, 4], BF16, name="te_g", tag="te_g", bufs=2, align_bytes=64)
+            nc.vector.tensor_copy(out=x[:], in_=wd.pop((g, c))[:].rearrange("p t n -> p n t"))
+            tg[g, c] = x
+
+        def te_quant(g, c):
+            nc.vector.quantize_mx(
+                out=te_c[g][c][:].bitcast(FP8X4), scales=te_s[g][c][:], in_=tg.pop((g, c))[:].rearrange("p n t -> p (n t)")
+            )
+
+        tags = ["o", "z", "o", "t", "o", "z", "o", "t"]
+
+        mo = {}
+
+        def mom_mm(c, j, g):
+            fg, tf = divmod(j, 4)
+            if g == 0:
+                mo[c, j] = bank(tags[j])
+            nc.tensor.matmul_mx(
+                out=mo[c, j][:],
+                lhsT=b_c[g][fg][:, tf * P : (tf + 1) * P].bitcast(FP8X4),
+                lhsT_scale=b_s[g][fg][:, tf * P : (tf + 1) * P],
+                rhs=te_c[g][c][:].bitcast(FP8X4),
+                rhs_scale=te_s[g][c][:],
+                start=(g == 0),
+                stop=(g == 1),
+            )
+
+        def mom_out(eng, c, j):
+            fg, tf = divmod(j, 4)
+            o = mo.pop((c, j))
+            r = work.tile([P, NB], F32, name="r1", tag="r1", bufs=12, align_bytes=64)
+            if eng is nc.vector:
+                nc.vector.tensor_copy(out=r[:], in_=o[:])
+            else:
+                nc.scalar.copy(out=r[:], in_=o[:])
+            nc.sync.dma_start(out=out1_v[fg, tf][:, c * NB : (c + 1) * NB], in_=r[:])
+
+        V, S = nc.vector, nc.scalar
+
+        emb_evac(0, 0, emb_transpose(0, 0, "t"))
+        w1_inter(S, 0, 0, 160)
+        w1_inter(V, 0, 160, 512)
+        emb_quant(0, 0)
+        w1_quant(0)
+        emb_evac(0, 1, emb_transpose(0, 1, "t"))
+        for i in range(2):
+            z_mm(i, 0)
+            silu(i, 0)
+        w1_inter(V, 1, 0, 512)
+        emb_quant(0, 1)
+        w1_quant(1)
+        for i in range(2):
+            h_transpose(i, 0)
+            a_mult(i, 0)
+            te_widen(V, 0, 0, 2 * i)
+            te_widen(V, 0, 0, 2 * i + 1)
+        for i in range(2):
+            z_mm(i, 1)
+            silu(i, 1)
+        for i in range(2):
+            h_transpose(i, 1)
+            a_mult(i, 1)
+        for fg in range(2):
+            z_mm(2, fg)
+            silu(2, fg)
+        a_quant(0)
+        te_inter(0, 0)
+        a_quant(1)
+        te_quant(0, 0)
+        bias_mm(0)
+        bias_out(0)
+        for fg in range(2):
+            z_mm(3, fg)
+            silu(3, fg)
+
+        first = {2: [lambda: emb_quant(1, 0)], 3: [lambda: b_quant(0, 0)], 4: [lambda: b_quant(0, 1)], 5: [lambda: te_quant(1, 0)], 6: [lambda: b_quant(1, 0)], 7: [lambda: b_quant(1, 1)]}
+        second = {2: [lambda: emb_quant(1, 1), lambda: b_mult(0, 0)], 3: [lambda: b_mult(0, 1)], 4: [lambda: te_inter(1, 0)], 5: [lambda: b_mult(1, 0)], 6: [lambda: b_mult(1, 1)], 7: [lambda: te_inter(0, 1)]}
+        wid = {2: (1, 0, 0), 3: (1, 0, 2), 4: (0, 1, 0), 5: (0, 1, 2), 6: (1, 1, 0), 7: (1, 1, 2)}
+        ahead = {2: [4], 3: [5, 6], 4: [7]}
+        for k in range(2, 9):
+            if k < 8:
+                for fg in range(2):
+                    h_transpose(k, fg)
+                    a_mult(k, fg)
+                if k == 2:
+                    emb_evac(1, 0, emb_transpose(1, 0, "o"), V.tensor_copy)
+                    emb_evac(1, 1, emb_transpose(1, 1, "o"), V.tensor_copy)
+                if k in wid:
+                    g, c, t = wid[k]
+                    te_widen(S, g, c, t)
+                    te_widen(S, g, c, t + 1)
+                for f in first.get(k, []):
+                    f()
+                a_quant(k)
+                for f in second.get(k, []):
+                    f()
+            bias_mm(k - 1)
+            bias_out(k - 1)
+            for i in ahead.get(k, []):
+                for fg in range(2):
+                    z_mm(i, fg)
+                    silu(i, fg)
+
+        prep = {
+            0: [
+                [lambda: te_quant(0, 1), lambda: te_inter(1, 1)],
+                [lambda: te_widen(V, 0, 2, 0), lambda: te_widen(S, 0, 2, 1)],
+                [lambda: te_quant(1, 1), lambda: te_widen(V, 0, 2, 2)],
+                [lambda: te_widen(S, 0, 2, 3)],
+                [lambda: te_inter(0, 2)],
+                [lambda: te_widen(V, 1, 2, 0), lambda: te_widen(S, 1, 2, 1)],
+                [lambda: te_quant(0, 2)],
+                [lambda: te_widen(V, 1, 2, 2), lambda: te_widen(S, 1, 2, 3)],
+            ],
+            1: [
+                [lambda: te_inter(1, 2)],
+                [lambda: te_quant(1, 2)],
+            ],
+        }
+        for c in range(NCH):
+            steps = prep.get(c, [])
+            if c == NCH - 1:
+                for j in range(8):
+                    mom_mm(c, j, 0)
+            for j in range(8):
+                if c < NCH - 1:
+                    mom_mm(c, j, 0)
+                mom_mm(c, j, 1)
+                if j < len(steps):
+                    for f in steps[j]:
+                        f()
+                on_vector = (c == 2 and j % 2 == 1) or (c == 1 and j in (4, 6))
+                mom_out(V if on_vector else S, c, j)

@@ -3,8 +3,8 @@ from contextlib import ExitStack
 import concourse.mybir as mybir
 from concourse.masks import make_identity
 
-M, K, F, PCOLS = 1024, 512, 1024, 1536
-FLOPS = 2 * M * K * F + 4 * M * F * PCOLS
+LEVELS, FEATURES, HIDDEN, COLS = 1024, 512, 1024, 1536
+FLOPS = 2 * LEVELS * FEATURES * HIDDEN + 2 * 2 * LEVELS * HIDDEN * COLS
 
 F32 = mybir.dt.float32
 BF16 = mybir.dt.bfloat16
@@ -18,350 +18,380 @@ ACT = mybir.ActivationFunctionType
 MULT = mybir.AluOpType.mult
 
 P = 128
-NB = 512
-NCH = PCOLS // NB
+T = 4
+GROUPS = 2
+BANK = 512
+CHUNKS = COLS // BANK
+TILES = GROUPS * T
+RUN = 8
+RUN_F32 = 4
 
 
 def tile_timestep_bias_table_calibration_s8_kernel(
-    tc, emb, w1, gain, table_words, table_scales, level_weight, teacher_bytes, teacher_scale, out_0, out_1
+    tc, emb, w1, gain, table_words, table_scales, level_weight, teacher_bytes, teacher_scale, bias, moments
 ):
     nc = tc.nc
+    sync, tensor, vector, scalar = nc.sync, nc.tensor, nc.vector, nc.scalar
+
     with ExitStack() as ctx:
         keep = ctx.enter_context(tc.tile_pool(name="keep", bufs=1))
         work = ctx.enter_context(tc.tile_pool(name="work", bufs=2))
         psum = ctx.enter_context(tc.psum_pool(name="psum", bufs=2))
         ctx.enter_context(tc.manual_schedule())
 
-        emb_raw = [keep.tile([P, 4, K], BF16, name="emb_raw%d" % g, align_bytes=64) for g in range(2)]
-        w1_raw = [keep.tile([P, 4, NB], BF16, name="w1_raw%d" % g, align_bytes=64) for g in range(2)]
-        w1_g = [keep.tile([P, NB, 4], BF16, name="w1_g%d" % g, align_bytes=64) for g in range(2)]
-        w1_c = [keep.tile([P, NB], U32, name="w1_c%d" % g, align_bytes=64) for g in range(2)]
-        w1_s = [keep.tile([P, NB], U8, name="w1_s%d" % g, align_bytes=64) for g in range(2)]
-        emb_g = [keep.tile([P, 4, P, 4], BF16, name="emb_g%d" % g, align_bytes=64) for g in range(2)]
-        emb_c = [keep.tile([P, 4 * P], U32, name="emb_c%d" % g, align_bytes=64) for g in range(2)]
-        emb_s = [keep.tile([P, 4 * P], U8, name="emb_s%d" % g, align_bytes=64) for g in range(2)]
-        h_sb = [[keep.tile([P, 4, NB], F32, name="h%d%d" % (g, fg), align_bytes=64) for fg in range(2)] for g in range(2)]
-        b_c = [[keep.tile([P, NB], U32, name="b_c%d%d" % (g, fg), align_bytes=64) for fg in range(2)] for g in range(2)]
-        b_s = [[keep.tile([P, NB], U8, name="b_s%d%d" % (g, fg), align_bytes=64) for fg in range(2)] for g in range(2)]
-        t_words = keep.tile([P, 2, 2 * PCOLS], U8, name="t_words", align_bytes=64)
-        t_scales = keep.tile([P, 2, PCOLS], U8, name="t_scales", align_bytes=64)
-        te_bytes = [keep.tile([P, 4, PCOLS], U8, name="te_bytes%d" % g, align_bytes=64) for g in range(2)]
-        te_c = [[keep.tile([P, NB], U32, name="te_c%d%d" % (g, c), align_bytes=64) for c in range(NCH)] for g in range(2)]
-        te_s = [[keep.tile([P, NB], U8, name="te_s%d%d" % (g, c), align_bytes=64) for c in range(NCH)] for g in range(2)]
-        gain_t = keep.tile([P, 2, 4], BF16, name="gain_t", align_bytes=64)
-        lw_t = keep.tile([P, 2, 4], BF16, name="lw_t", align_bytes=64)
-        ts_t = keep.tile([P, 2, 4], F32, name="ts_t", align_bytes=64)
-        ident = keep.tile([P, P], F32, name="ident", align_bytes=64)
-        warm = keep.tile([P, 8], F32, name="warm", align_bytes=64)
+        def kept(name, shape, dtype):
+            return keep.tile([P] + shape, dtype, name=name, align_bytes=64)
 
-        emb_v = emb.rearrange("(g p t) k -> g p t k", p=P, t=4)
-        w1_v = w1.rearrange("(p j) f -> p j f", j=4)
-        te_v = teacher_bytes.rearrange("(g p t) c -> g p t c", p=P, t=4)
-        out0_v = out_0.rearrange("(g p t) c -> g t p c", p=P, t=4)
-        out1_v = out_1.rearrange("(g p t) c -> g t p c", p=P, t=4)
+        def per_group(name, shape, dtype):
+            return [kept("%s%d" % (name, g), shape, dtype) for g in range(GROUPS)]
 
-        nc.gpsimd.memset(warm[:], 0.0)
-        nc.scalar.dma_start(out=gain_t[:], in_=gain.rearrange("(g p t) -> p g t", p=P, t=4))
-        nc.scalar.dma_start(out=lw_t[:], in_=level_weight.rearrange("(g p t) -> p g t", p=P, t=4))
-        nc.scalar.dma_start(out=ts_t[:], in_=teacher_scale.rearrange("(g p t) o -> p g (t o)", p=P, t=4))
-        nc.scalar.activation(out=warm[:, 0:1], in_=warm[:, 1:2], func=ACT.Silu)
-        make_identity(nc, ident[:])
-        nc.vector.memset(t_scales[:].rearrange("p g n -> p (g n)").bitcast(I32), 0)
+        emb_rows = per_group("emb_rows", [T, FEATURES], BF16)
+        emb_mixed = per_group("emb_mixed", [T, P, T], BF16)
+        emb_codes = per_group("emb_codes", [T * P], U32)
+        emb_scales = per_group("emb_scales", [T * P], U8)
+        w1_rows = per_group("w1_rows", [T, BANK], BF16)
+        w1_mixed = per_group("w1_mixed", [BANK, T], BF16)
+        w1_codes = per_group("w1_codes", [BANK], U32)
+        w1_scales = per_group("w1_scales", [BANK], U8)
+        h = [per_group("h%d" % g, [T, BANK], F32) for g in range(GROUPS)]
+        b_codes = [per_group("b_codes%d" % g, [BANK], U32) for g in range(GROUPS)]
+        b_scales = [per_group("b_scales%d" % g, [BANK], U8) for g in range(GROUPS)]
+        t_words = kept("t_words", [GROUPS, 2 * COLS], U8)
+        t_scales = kept("t_scales", [GROUPS, COLS], U8)
+        teach_bytes = per_group("teach_bytes", [T, COLS], U8)
+        teach_codes = [[kept("teach_codes%d%d" % (g, c), [BANK], U32) for c in range(CHUNKS)] for g in range(GROUPS)]
+        teach_scales = [[kept("teach_scales%d%d" % (g, c), [BANK], U8) for c in range(CHUNKS)] for g in range(GROUPS)]
+        gain_col = kept("gain_col", [GROUPS, T], BF16)
+        weight_col = kept("weight_col", [GROUPS, T], BF16)
+        factor_col = kept("factor_col", [GROUPS, T], F32)
+        identity = kept("identity", [P], F32)
+        dummy = kept("dummy", [8], F32)
+
+        emb_hbm = emb.rearrange("(g p t) k -> g p t k", p=P, t=T)
+        w1_hbm = w1.rearrange("(p t) n -> p t n", t=T)
+        teach_hbm = teacher_bytes.rearrange("(g p t) c -> g p t c", p=P, t=T)
+        bias_hbm = bias.rearrange("(g p t) c -> g t p c", p=P, t=T)
+        moments_hbm = moments.rearrange("(g p t) c -> g t p c", p=P, t=T)
+
+        def load_w1(f):
+            sync.dma_start(out=w1_rows[f][:], in_=w1_hbm[:, :, f * BANK : (f + 1) * BANK])
+
+        def load_emb(g, t0, t1):
+            sync.dma_start(out=emb_rows[g][:, t0:t1, :], in_=emb_hbm[g][:, t0:t1, :])
 
         def load_teacher(g, c0, c1):
-            cols = slice(c0 * NB, c1 * NB)
-            nc.sync.dma_start(out=te_bytes[g][:, :, cols], in_=te_v[g][:, :, cols])
+            cols = slice(c0 * BANK, c1 * BANK)
+            sync.dma_start(out=teach_bytes[g][:, :, cols], in_=teach_hbm[g][:, :, cols])
 
-        nc.sync.dma_start(out=emb_raw[0][:, 0:2, :], in_=emb_v[0][:, 0:2, :])
-        nc.sync.dma_start(out=w1_raw[0][:], in_=w1_v[:, :, 0:NB])
-        nc.sync.dma_start(out=emb_raw[0][:, 2:4, :], in_=emb_v[0][:, 2:4, :])
-        nc.sync.dma_start(out=w1_raw[1][:], in_=w1_v[:, :, NB:F])
+        nc.gpsimd.memset(dummy[:], 0.0)
+        scalar.dma_start(out=gain_col[:], in_=gain.rearrange("(g p t) -> p g t", p=P, t=T))
+        scalar.dma_start(out=weight_col[:], in_=level_weight.rearrange("(g p t) -> p g t", p=P, t=T))
+        scalar.dma_start(out=factor_col[:], in_=teacher_scale.rearrange("(g p t) o -> p g (t o)", p=P, t=T))
+        scalar.activation(out=dummy[:, 0:1], in_=dummy[:, 1:2], func=ACT.Silu)
+        make_identity(nc, identity[:])
+        vector.memset(t_scales[:].rearrange("p g n -> p (g n)").bitcast(I32), 0)
+
+        load_w1(0)
+        load_emb(0, 0, 2)
+        load_emb(0, 2, 4)
+        load_w1(1)
         load_teacher(0, 0, 1)
-        for g in range(2):
-            nc.sync.dma_start(out=t_words[:, g, :].bitcast(I32), in_=table_words[g].bitcast(I32))
+        for g in range(GROUPS):
+            sync.dma_start(out=t_words[:, g, :].bitcast(I32), in_=table_words[g].bitcast(I32))
         for q in range(4):
-            nc.sync.dma_start(
+            sync.dma_start(
                 out=t_scales[32 * q : 32 * q + 4, :, :].bitcast(I32),
                 in_=table_scales[:, 4 * q : 4 * q + 4, :].rearrange("g q n -> q g n").bitcast(I32),
             )
-        nc.sync.dma_start(out=emb_raw[1][:], in_=emb_v[1])
+        load_emb(1, 0, 4)
         load_teacher(1, 0, 1)
-        load_teacher(0, 1, 3)
-        load_teacher(1, 1, 3)
+        load_teacher(0, 1, CHUNKS)
+        load_teacher(1, 1, CHUNKS)
 
-        def bank(tag):
-            return psum.tile([P, NB], F32, name="ps_" + tag, tag=tag, bufs=4 if tag == "o" else 2)
+        BANKS = {"z": 2, "turned": 2, "rest": 4}
 
-        def emb_transpose(g, half, tag):
-            xt = bank(tag)
-            for tt in range(2):
-                words = emb_raw[g][:, 2 * half + tt, :].bitcast(F32)
-                for u in range(2):
-                    at = (2 * tt + u) * P
-                    nc.tensor.transpose(xt[:, at : at + P], words[:, u : K // 2 : 2], ident[:])
-            return xt
+        def new_bank(tag):
+            return psum.tile([P, BANK], F32, name="bank_" + tag, tag=tag, bufs=BANKS[tag])
 
-        def emb_evac(g, half, xt, copy=nc.scalar.copy):
-            copy(
-                out=emb_g[g][:, 2 * half : 2 * half + 2, :, :].rearrange("p t r k -> p t (r k)").bitcast(F32).rearrange("p t (r u) -> p t r u", u=2),
-                in_=xt[:].rearrange("p (t u r) -> p t r u", t=2, u=2),
-            )
+        def new_work(tag, shape, dtype, bufs):
+            return work.tile([P] + shape, dtype, name=tag, tag=tag, bufs=bufs, align_bytes=64)
 
-        def emb_quant(g, half):
-            cols = slice(2 * half * P, (2 * half + 2) * P)
-            nc.vector.quantize_mx(
-                out=emb_c[g][:, cols].bitcast(FP8X4),
-                scales=emb_s[g][:, cols],
-                in_=emb_g[g][:, 2 * half : 2 * half + 2, :, :].rearrange("p t r k -> p (t r k)"),
-            )
-
-        def w1_inter(eng, fg, c0, c1):
-            o = w1_g[fg][:, c0:c1, :]
-            i = w1_raw[fg][:, :, c0:c1].rearrange("p j w -> p w j")
-            if eng is nc.vector:
-                nc.vector.tensor_copy(out=o, in_=i)
+        def copy(engine, out, in_):
+            if engine is scalar:
+                scalar.copy(out=out, in_=in_)
             else:
-                nc.scalar.copy(out=o, in_=i)
+                vector.tensor_copy(out=out, in_=in_)
 
-        def w1_quant(fg):
-            nc.vector.quantize_mx(
-                out=w1_c[fg][:].bitcast(FP8X4), scales=w1_s[fg][:], in_=w1_g[fg][:].rearrange("p w j -> p (w j)")
+        def quantize(codes, scales, values):
+            vector.quantize_mx(out=codes.bitcast(FP8X4), scales=scales, in_=values)
+
+        def interleave(engine, out, rows):
+            copy(
+                engine,
+                out.rearrange("p (c i) t -> p c t i", i=RUN),
+                rows.rearrange("p t (c i) -> p c t i", i=RUN),
             )
 
-        zb = {}
-        tb = {}
-        ag = {}
-        ac = {}
-        ob = {}
-        wd = {}
-        tg = {}
+        def emb_turn(g, half, tag):
+            turned = new_bank(tag)
+            for s in range(2):
+                words = emb_rows[g][:, 2 * half + s, :].bitcast(F32)
+                for u in range(2):
+                    at = (2 * s + u) * P
+                    tensor.transpose(turned[:, at : at + P], words[:, u : FEATURES // 2 : 2], identity[:])
+            return turned
 
-        def z_mm(i, fg):
-            g, t = divmod(i, 4)
-            z = bank("z")
-            nc.tensor.matmul_mx(
-                out=z[:],
-                lhsT=emb_c[g][:, t * P : (t + 1) * P].bitcast(FP8X4),
-                lhsT_scale=emb_s[g][:, t * P : (t + 1) * P],
-                rhs=w1_c[fg][:].bitcast(FP8X4),
-                rhs_scale=w1_s[fg][:],
+        def emb_interleave(engine, g, half, turned):
+            pair = emb_mixed[g][:, 2 * half : 2 * half + 2, :, :].rearrange("p v r k -> p v (r k)")
+            copy(
+                engine,
+                pair.bitcast(F32).rearrange("p v (r u) -> p v r u", u=2),
+                turned[:].rearrange("p (v u r) -> p v r u", v=2, u=2),
+            )
+
+        def emb_quantize(g, half):
+            cols = slice(2 * half * P, (2 * half + 2) * P)
+            values = emb_mixed[g][:, 2 * half : 2 * half + 2, :, :].rearrange("p v r k -> p (v r k)")
+            quantize(emb_codes[g][:, cols], emb_scales[g][:, cols], values)
+
+        def w1_interleave(engine, f, n0, n1):
+            interleave(engine, w1_mixed[f][:, n0:n1, :], w1_rows[f][:, :, n0:n1])
+
+        def w1_quantize(f):
+            quantize(w1_codes[f][:], w1_scales[f][:], w1_mixed[f][:].rearrange("p n t -> p (n t)"))
+
+        z_bank = {}
+
+        def z_matmul(i, f):
+            g, t = divmod(i, T)
+            z_bank[i, f] = new_bank("z")
+            tensor.matmul_mx(
+                out=z_bank[i, f][:],
+                lhsT=emb_codes[g][:, t * P : (t + 1) * P].bitcast(FP8X4),
+                lhsT_scale=emb_scales[g][:, t * P : (t + 1) * P],
+                rhs=w1_codes[f][:].bitcast(FP8X4),
+                rhs_scale=w1_scales[f][:],
                 start=True,
                 stop=True,
             )
-            zb[i, fg] = z
 
-        def silu(i, fg):
-            g, t = divmod(i, 4)
-            nc.scalar.activation(
-                out=h_sb[g][fg][:, t, :].rearrange("p (t m) -> p t m", t=4),
-                in_=zb.pop((i, fg))[:].rearrange("p (m t) -> p t m", t=4),
+        def silu(i, f):
+            g, t = divmod(i, T)
+            scalar.activation(
+                out=h[g][f][:, t, :].rearrange("p (t c) -> p t c", t=T),
+                in_=z_bank.pop((i, f))[:].rearrange("p (c t) -> p t c", t=T),
                 func=ACT.Silu,
             )
 
-        def h_transpose(i, fg):
-            g, t = divmod(i, 4)
-            x = bank("t")
-            for tf in range(4):
-                nc.tensor.transpose(x[:, tf * P : (tf + 1) * P], h_sb[g][fg][:, t, tf * P : (tf + 1) * P], ident[:])
-            tb[i, fg] = x
+        h_turned = {}
+        a_mixed = {}
+        a_quantized = {}
+        bias_bank = {}
+        bias_rows = {}
 
-        def a_mult(i, fg):
-            if i not in ag:
-                ag[i] = work.tile([P, 2, P, 4], BF16, name="a_g", tag="a_g", bufs=3, align_bytes=64)
-            nc.vector.tensor_tensor(
-                out=ag[i][:, fg, :, :],
-                in0=tb.pop((i, fg))[:].rearrange("p (t m) -> p m t", t=4),
-                in1=gain_t[:, fg, :].unsqueeze(1).to_broadcast([P, P, 4]),
+        def h_turn(i, f):
+            g, t = divmod(i, T)
+            h_turned[i, f] = new_bank("turned")
+            for s in range(T):
+                cols = slice(s * P, (s + 1) * P)
+                tensor.transpose(h_turned[i, f][:, cols], h[g][f][:, t, cols], identity[:])
+
+        def a_multiply(i, f):
+            if i not in a_mixed:
+                a_mixed[i] = new_work("a_mixed", [GROUPS, P, T], BF16, 3)
+            vector.tensor_tensor(
+                out=a_mixed[i][:, f, :, :],
+                in0=h_turned.pop((i, f))[:].rearrange("p (t r) -> p r t", t=T),
+                in1=gain_col[:, f, :].unsqueeze(1).to_broadcast([P, P, T]),
                 op=MULT,
             )
 
-        def a_quant(i):
-            c = work.tile([P, 2 * P], U32, name="a_c", tag="a_c", bufs=3, align_bytes=64)
-            s = work.tile([P, 2 * P], U8, name="a_s", tag="a_s", bufs=3, align_bytes=64)
-            nc.vector.quantize_mx(out=c[:].bitcast(FP8X4), scales=s[:], in_=ag.pop(i)[:].rearrange("p g m t -> p (g m t)"))
-            ac[i] = (c, s)
+        def a_quantize(i):
+            codes = new_work("a_codes", [GROUPS * P], U32, 3)
+            scales = new_work("a_scales", [GROUPS * P], U8, 3)
+            quantize(codes[:], scales[:], a_mixed.pop(i)[:].rearrange("p f r t -> p (f r t)"))
+            a_quantized[i] = (codes, scales)
 
-        def bias_mm(i):
-            c, s = ac.pop(i)
-            for n in range(NCH):
-                o = bank("o")
-                for fg in range(2):
-                    nc.tensor.matmul_mx(
-                        out=o[:],
-                        lhsT=c[:, fg * P : (fg + 1) * P].bitcast(FP8X4),
-                        lhsT_scale=s[:, fg * P : (fg + 1) * P],
-                        rhs=t_words[:, fg, 2 * NB * n : 2 * NB * (n + 1)].bitcast(FP4X4),
-                        rhs_scale=t_scales[:, fg, NB * n : NB * (n + 1)],
-                        start=(fg == 0),
-                        stop=(fg == 1),
-                    )
-                ob[i, n] = o
+        def bias_matmul(i, c):
+            codes, scales = a_quantized[i]
+            bias_bank[i, c] = new_bank("rest")
+            for f in range(GROUPS):
+                tensor.matmul_mx(
+                    out=bias_bank[i, c][:],
+                    lhsT=codes[:, f * P : (f + 1) * P].bitcast(FP8X4),
+                    lhsT_scale=scales[:, f * P : (f + 1) * P],
+                    rhs=t_words[:, f, 2 * BANK * c : 2 * BANK * (c + 1)].bitcast(FP4X4),
+                    rhs_scale=t_scales[:, f, BANK * c : BANK * (c + 1)],
+                    start=(f == 0),
+                    stop=(f == GROUPS - 1),
+                )
 
-        def bias_out(i):
-            g, t = divmod(i, 4)
-            r = work.tile([P, PCOLS], F32, name="r0", tag="r0", bufs=4, align_bytes=64)
-            for n in range(NCH):
-                nc.scalar.copy(out=r[:, n * NB : (n + 1) * NB], in_=ob.pop((i, n))[:])
-            nc.sync.dma_start(out=out0_v[g, t], in_=r[:])
+        def bias_out(i, c):
+            g, t = divmod(i, T)
+            if c == 0:
+                bias_rows[i] = new_work("bias_rows", [COLS], F32, 4)
+            scalar.copy(out=bias_rows[i][:, c * BANK : (c + 1) * BANK], in_=bias_bank.pop((i, c))[:])
+            if c == CHUNKS - 1:
+                sync.dma_start(out=bias_hbm[g, t], in_=bias_rows.pop(i)[:])
 
-        bgs = {}
+        b_mixed = {}
 
-        def b_mult(g, fg):
-            bt = work.tile([P, NB, 4], BF16, name="b_g", tag="b_g", bufs=2, align_bytes=64)
-            nc.vector.tensor_tensor(
-                out=bt[:],
-                in0=h_sb[g][fg][:].rearrange("p t f -> p f t"),
-                in1=lw_t[:, g, :].unsqueeze(1).to_broadcast([P, NB, 4]),
+        def b_multiply(g, f):
+            b_mixed[g, f] = new_work("b_mixed", [BANK, T], BF16, 2)
+            runs = BANK // RUN_F32
+            vector.tensor_tensor(
+                out=b_mixed[g, f][:].rearrange("p (c i) t -> p c t i", i=RUN_F32),
+                in0=h[g][f][:].rearrange("p t (c i) -> p c t i", i=RUN_F32),
+                in1=weight_col[:, g, :].unsqueeze(1).unsqueeze(3).to_broadcast([P, runs, T, RUN_F32]),
                 op=MULT,
             )
-            bgs[g, fg] = bt
 
-        def b_quant(g, fg):
-            nc.vector.quantize_mx(
-                out=b_c[g][fg][:].bitcast(FP8X4), scales=b_s[g][fg][:], in_=bgs.pop((g, fg))[:].rearrange("p f t -> p (f t)")
-            )
+        def b_quantize(g, f):
+            quantize(b_codes[g][f][:], b_scales[g][f][:], b_mixed.pop((g, f))[:].rearrange("p n t -> p (n t)"))
 
-        def te_widen(eng, g, c, t):
-            if t == 0:
-                wd[g, c] = work.tile([P, 4, NB], BF16, name="wide", tag="wide", bufs=3, align_bytes=64)
-            o = wd[g, c][:, t, :]
-            i = te_bytes[g][:, t, c * NB : (c + 1) * NB].bitcast(FP8)
-            if eng is nc.vector:
-                nc.vector.tensor_scalar(out=o, in0=i, scalar1=ts_t[:, g, t : t + 1], scalar2=None, op0=MULT)
+        wide = {}
+        teach_mixed = {}
+
+        def widen(engine, g, c, t):
+            if (g, c) not in wide:
+                wide[g, c] = new_work("wide", [T, BANK], BF16, 3)
+            out = wide[g, c][:, t, :]
+            values = teach_bytes[g][:, t, c * BANK : (c + 1) * BANK].bitcast(FP8)
+            factor = factor_col[:, g, t : t + 1]
+            if engine is scalar:
+                scalar.activation(out=out, in_=values, func=ACT.Copy, scale=factor)
             else:
-                nc.scalar.activation(out=o, in_=i, func=ACT.Copy, scale=ts_t[:, g, t : t + 1])
+                vector.tensor_scalar(out=out, in0=values, scalar1=factor, scalar2=None, op0=MULT)
 
-        def te_inter(g, c):
-            x = work.tile([P, NB, 4], BF16, name="te_g", tag="te_g", bufs=2, align_bytes=64)
-            nc.vector.tensor_copy(out=x[:], in_=wd.pop((g, c))[:].rearrange("p t n -> p n t"))
-            tg[g, c] = x
+        def teach_interleave(g, c):
+            teach_mixed[g, c] = new_work("teach_mixed", [BANK, T], BF16, 2)
+            interleave(vector, teach_mixed[g, c][:], wide.pop((g, c))[:])
 
-        def te_quant(g, c):
-            nc.vector.quantize_mx(
-                out=te_c[g][c][:].bitcast(FP8X4), scales=te_s[g][c][:], in_=tg.pop((g, c))[:].rearrange("p n t -> p (n t)")
-            )
+        def teach_quantize(g, c):
+            quantize(teach_codes[g][c][:], teach_scales[g][c][:], teach_mixed.pop((g, c))[:].rearrange("p n t -> p (n t)"))
 
-        tags = ["o", "z", "o", "t", "o", "z", "o", "t"]
+        def moments_matmul(c, j):
+            f, s = divmod(j, T)
+            bank = new_bank(["rest", "z", "rest", "turned"][j % 4])
+            for g in range(GROUPS):
+                tensor.matmul_mx(
+                    out=bank[:],
+                    lhsT=b_codes[g][f][:, s * P : (s + 1) * P].bitcast(FP8X4),
+                    lhsT_scale=b_scales[g][f][:, s * P : (s + 1) * P],
+                    rhs=teach_codes[g][c][:].bitcast(FP8X4),
+                    rhs_scale=teach_scales[g][c][:],
+                    start=(g == 0),
+                    stop=(g == GROUPS - 1),
+                )
+            return bank
 
-        mo = {}
+        def moments_out(engine, c, j, bank):
+            f, s = divmod(j, T)
+            rows = new_work("moment_rows", [BANK], F32, 12)
+            copy(engine, rows[:], bank[:])
+            sync.dma_start(out=moments_hbm[f, s][:, c * BANK : (c + 1) * BANK], in_=rows[:])
 
-        def mom_mm(c, j, g):
-            fg, tf = divmod(j, 4)
-            if g == 0:
-                mo[c, j] = bank(tags[j])
-            nc.tensor.matmul_mx(
-                out=mo[c, j][:],
-                lhsT=b_c[g][fg][:, tf * P : (tf + 1) * P].bitcast(FP8X4),
-                lhsT_scale=b_s[g][fg][:, tf * P : (tf + 1) * P],
-                rhs=te_c[g][c][:].bitcast(FP8X4),
-                rhs_scale=te_s[g][c][:],
-                start=(g == 0),
-                stop=(g == 1),
-            )
 
-        def mom_out(eng, c, j):
-            fg, tf = divmod(j, 4)
-            o = mo.pop((c, j))
-            r = work.tile([P, NB], F32, name="r1", tag="r1", bufs=12, align_bytes=64)
-            if eng is nc.vector:
-                nc.vector.tensor_copy(out=r[:], in_=o[:])
-            else:
-                nc.scalar.copy(out=r[:], in_=o[:])
-            nc.sync.dma_start(out=out1_v[fg, tf][:, c * NB : (c + 1) * NB], in_=r[:])
+        w1_interleave(scalar, 0, 352, BANK)
+        w1_interleave(vector, 0, 0, 352)
+        emb_interleave(scalar, 0, 0, emb_turn(0, 0, "turned"))
+        w1_quantize(0)
+        emb_quantize(0, 0)
+        emb_interleave(scalar, 0, 1, emb_turn(0, 1, "turned"))
+        z_matmul(0, 0)
+        z_matmul(1, 0)
+        emb_quantize(0, 1)
+        w1_interleave(scalar, 1, 0, 128)
+        w1_interleave(vector, 1, 128, BANK)
+        silu(0, 0)
+        silu(1, 0)
+        widen(vector, 0, 0, 0)
+        w1_quantize(1)
+        widen(scalar, 0, 0, 3)
+        h_turn(0, 0)
+        widen(vector, 0, 0, 1)
+        widen(vector, 0, 0, 2)
+        z_matmul(0, 1)
+        z_matmul(1, 1)
+        silu(0, 1)
+        silu(1, 1)
+        h_turn(1, 0)
+        a_multiply(0, 0)
+        teach_interleave(0, 0)
+        a_multiply(1, 0)
+        h_turn(0, 1)
+        a_multiply(0, 1)
+        for f in range(GROUPS):
+            z_matmul(2, f)
+            silu(2, f)
+        turned = [emb_turn(1, half, "rest") for half in range(2)]
+        for half in range(2):
+            emb_interleave(scalar, 1, half, turned[half])
+        teach_quantize(0, 0)
+        a_quantize(0)
+        h_turn(1, 1)
+        a_multiply(1, 1)
+        for f in range(GROUPS):
+            z_matmul(3, f)
+            silu(3, f)
+        emb_quantize(1, 0)
+        a_quantize(1)
+        for f in range(GROUPS):
+            h_turn(2, f)
+            a_multiply(2, f)
+        widen(scalar, 1, 0, 0)
+        for f in range(GROUPS):
+            z_matmul(4, f)
+            silu(4, f)
+        b_multiply(0, 0)
 
-        V, S = nc.vector, nc.scalar
-
-        emb_evac(0, 0, emb_transpose(0, 0, "t"))
-        w1_inter(S, 0, 0, 160)
-        w1_inter(V, 0, 160, 512)
-        emb_quant(0, 0)
-        w1_quant(0)
-        emb_evac(0, 1, emb_transpose(0, 1, "t"))
-        for i in range(2):
-            z_mm(i, 0)
-            silu(i, 0)
-        w1_inter(V, 1, 0, 512)
-        emb_quant(0, 1)
-        w1_quant(1)
-        for i in range(2):
-            h_transpose(i, 0)
-            a_mult(i, 0)
-            te_widen(V, 0, 0, 2 * i)
-            te_widen(V, 0, 0, 2 * i + 1)
-        for i in range(2):
-            z_mm(i, 1)
-            silu(i, 1)
-        for i in range(2):
-            h_transpose(i, 1)
-            a_mult(i, 1)
-        for fg in range(2):
-            z_mm(2, fg)
-            silu(2, fg)
-        a_quant(0)
-        te_inter(0, 0)
-        a_quant(1)
-        te_quant(0, 0)
-        bias_mm(0)
-        bias_out(0)
-        for fg in range(2):
-            z_mm(3, fg)
-            silu(3, fg)
-
-        first = {2: [lambda: emb_quant(1, 0)], 3: [lambda: b_quant(0, 0)], 4: [lambda: b_quant(0, 1)], 5: [lambda: te_quant(1, 0)], 6: [lambda: b_quant(1, 0)], 7: [lambda: b_quant(1, 1)]}
-        second = {2: [lambda: emb_quant(1, 1), lambda: b_mult(0, 0)], 3: [lambda: b_mult(0, 1)], 4: [lambda: te_inter(1, 0)], 5: [lambda: b_mult(1, 0)], 6: [lambda: b_mult(1, 1)], 7: [lambda: te_inter(0, 1)]}
-        wid = {2: (1, 0, 0), 3: (1, 0, 2), 4: (0, 1, 0), 5: (0, 1, 2), 6: (1, 1, 0), 7: (1, 1, 2)}
-        ahead = {2: [4], 3: [5, 6], 4: [7]}
-        for k in range(2, 9):
-            if k < 8:
-                for fg in range(2):
-                    h_transpose(k, fg)
-                    a_mult(k, fg)
-                if k == 2:
-                    emb_evac(1, 0, emb_transpose(1, 0, "o"), V.tensor_copy)
-                    emb_evac(1, 1, emb_transpose(1, 1, "o"), V.tensor_copy)
-                if k in wid:
-                    g, c, t = wid[k]
-                    te_widen(S, g, c, t)
-                    te_widen(S, g, c, t + 1)
-                for f in first.get(k, []):
-                    f()
-                a_quant(k)
-                for f in second.get(k, []):
-                    f()
-            bias_mm(k - 1)
-            bias_out(k - 1)
-            for i in ahead.get(k, []):
-                for fg in range(2):
-                    z_mm(i, fg)
-                    silu(i, fg)
-
-        prep = {
-            0: [
-                [lambda: te_quant(0, 1), lambda: te_inter(1, 1)],
-                [lambda: te_widen(V, 0, 2, 0), lambda: te_widen(S, 0, 2, 1)],
-                [lambda: te_quant(1, 1), lambda: te_widen(V, 0, 2, 2)],
-                [lambda: te_widen(S, 0, 2, 3)],
-                [lambda: te_inter(0, 2)],
-                [lambda: te_widen(V, 1, 2, 0), lambda: te_widen(S, 1, 2, 1)],
-                [lambda: te_quant(0, 2)],
-                [lambda: te_widen(V, 1, 2, 2), lambda: te_widen(S, 1, 2, 3)],
-            ],
-            1: [
-                [lambda: te_inter(1, 2)],
-                [lambda: te_quant(1, 2)],
-            ],
+        bias_tiles = {3: [0], 4: [1, 2], 5: [3, 4], 6: [5], 7: [6, 7]}
+        vector_work = {
+            3: [(emb_quantize, 1, 1), (a_quantize, 2)],
+            4: [(a_quantize, 3), (b_multiply, 0, 1), (a_quantize, 4), (widen, vector, 1, 0, 3), (b_quantize, 0, 0)],
+            5: [(b_quantize, 0, 1), (a_quantize, 5)],
+            6: [(teach_interleave, 1, 0), (a_quantize, 6), (b_multiply, 1, 0)],
+            7: [(teach_quantize, 1, 0), (a_quantize, 7), (b_quantize, 1, 0), (b_multiply, 1, 1), (b_quantize, 1, 1)],
         }
-        for c in range(NCH):
-            steps = prep.get(c, [])
-            if c == NCH - 1:
-                for j in range(8):
-                    mom_mm(c, j, 0)
-            for j in range(8):
-                if c < NCH - 1:
-                    mom_mm(c, j, 0)
-                mom_mm(c, j, 1)
-                if j < len(steps):
-                    for f in steps[j]:
-                        f()
-                on_vector = (c == 2 and j % 2 == 1) or (c == 1 and j in (4, 6))
-                mom_out(V if on_vector else S, c, j)
+        scalar_widens = {0: (1, 0, 1), 1: (1, 0, 2), 5: (1, 1, 0), 6: (0, 1, 0), 7: (0, 1, 1)}
+        for k in range(3, TILES):
+            if k not in (5, 6):
+                for f in range(GROUPS):
+                    h_turn(k, f)
+            for f in range(GROUPS):
+                a_multiply(k, f)
+            for piece, *args in vector_work[k]:
+                piece(*args)
+            for i in bias_tiles[k]:
+                if i in (2, 4):
+                    for f in range(GROUPS):
+                        h_turn(k + 1, f)
+                for c in range(CHUNKS):
+                    bias_matmul(i, c)
+                    bias_out(i, c)
+                    if i < 3 and c < GROUPS:
+                        z_matmul(i + 5, c)
+                        silu(i + 5, c)
+                if i in scalar_widens:
+                    widen(scalar, *scalar_widens[i])
+
+        teacher_work = {
+            (0, 0): [(widen, vector, 1, 1, 1), (widen, vector, 1, 1, 2), (widen, vector, 1, 1, 3), (teach_interleave, 1, 1)],
+            (0, 1): [(widen, scalar, 0, 1, 2), (widen, vector, 0, 1, 3)],
+            (0, 2): [(teach_quantize, 1, 1), (teach_interleave, 0, 1)],
+            (0, 3): [(widen, scalar, 0, 2, 0)],
+            (0, 4): [(widen, vector, 0, 2, 1), (teach_quantize, 0, 1), (widen, vector, 0, 2, 2), (widen, vector, 0, 2, 3)],
+            (0, 5): [(widen, vector, 1, 2, 1), (widen, vector, 1, 2, 2)],
+            (0, 6): [(teach_interleave, 0, 2)],
+            (0, 7): [(widen, scalar, 1, 2, 0)],
+            (1, 0): [(widen, vector, 1, 2, 3), (teach_quantize, 0, 2)],
+            (1, 1): [(teach_interleave, 1, 2)],
+            (1, 2): [(teach_quantize, 1, 2)],
+        }
+        for c in range(CHUNKS):
+            for j in range(TILES):
+                bank = moments_matmul(c, j)
+                for piece, *args in teacher_work.get((c, j), []):
+                    piece(*args)
+                engine = vector if c == CHUNKS - 1 and j % 2 == 0 else scalar
+                moments_out(engine, c, j, bank)

from contextlib import ExitStack

import concourse.mybir as mybir
from concourse.masks import make_identity

LEVELS, FEATURES, HIDDEN, COLS = 1024, 512, 1024, 1536
FLOPS = 2 * LEVELS * FEATURES * HIDDEN + 2 * 2 * LEVELS * HIDDEN * COLS

F32 = mybir.dt.float32
BF16 = mybir.dt.bfloat16
I32 = mybir.dt.int32
U32 = mybir.dt.uint32
U8 = mybir.dt.uint8
FP8 = mybir.dt.float8_e4m3fn
FP8X4 = mybir.dt.float8_e4m3fn_x4
FP4X4 = mybir.dt.float4_e2m1fn_x4
ACT = mybir.ActivationFunctionType
MULT = mybir.AluOpType.mult

P = 128
T = 4
GROUPS = 2
BANK = 512
CHUNKS = COLS // BANK
TILES = GROUPS * T
RUN = 8
RUN_F32 = 4


def tile_timestep_bias_table_calibration_s8_kernel(
    tc, emb, w1, gain, table_words, table_scales, level_weight, teacher_bytes, teacher_scale, bias, moments
):
    nc = tc.nc
    sync, tensor, vector, scalar = nc.sync, nc.tensor, nc.vector, nc.scalar

    with ExitStack() as ctx:
        keep = ctx.enter_context(tc.tile_pool(name="keep", bufs=1))
        work = ctx.enter_context(tc.tile_pool(name="work", bufs=2))
        psum = ctx.enter_context(tc.psum_pool(name="psum", bufs=2))
        ctx.enter_context(tc.manual_schedule())

        def kept(name, shape, dtype):
            return keep.tile([P] + shape, dtype, name=name, align_bytes=64)

        def per_group(name, shape, dtype):
            return [kept("%s%d" % (name, g), shape, dtype) for g in range(GROUPS)]

        emb_rows = per_group("emb_rows", [T, FEATURES], BF16)
        emb_mixed = per_group("emb_mixed", [T, P, T], BF16)
        emb_codes = per_group("emb_codes", [T * P], U32)
        emb_scales = per_group("emb_scales", [T * P], U8)
        w1_rows = per_group("w1_rows", [T, BANK], BF16)
        w1_mixed = per_group("w1_mixed", [BANK, T], BF16)
        w1_codes = per_group("w1_codes", [BANK], U32)
        w1_scales = per_group("w1_scales", [BANK], U8)
        h = [per_group("h%d" % g, [T, BANK], F32) for g in range(GROUPS)]
        b_codes = [per_group("b_codes%d" % g, [BANK], U32) for g in range(GROUPS)]
        b_scales = [per_group("b_scales%d" % g, [BANK], U8) for g in range(GROUPS)]
        t_words = kept("t_words", [GROUPS, 2 * COLS], U8)
        t_scales = kept("t_scales", [GROUPS, COLS], U8)
        teach_bytes = per_group("teach_bytes", [T, COLS], U8)
        teach_codes = [[kept("teach_codes%d%d" % (g, c), [BANK], U32) for c in range(CHUNKS)] for g in range(GROUPS)]
        teach_scales = [[kept("teach_scales%d%d" % (g, c), [BANK], U8) for c in range(CHUNKS)] for g in range(GROUPS)]
        gain_col = kept("gain_col", [GROUPS, T], BF16)
        weight_col = kept("weight_col", [GROUPS, T], BF16)
        factor_col = kept("factor_col", [GROUPS, T], F32)
        identity = kept("identity", [P], F32)
        dummy = kept("dummy", [8], F32)

        emb_hbm = emb.rearrange("(g p t) k -> g p t k", p=P, t=T)
        w1_hbm = w1.rearrange("(p t) n -> p t n", t=T)
        teach_hbm = teacher_bytes.rearrange("(g p t) c -> g p t c", p=P, t=T)
        bias_hbm = bias.rearrange("(g p t) c -> g t p c", p=P, t=T)
        moments_hbm = moments.rearrange("(g p t) c -> g t p c", p=P, t=T)

        def load_w1(f):
            sync.dma_start(out=w1_rows[f][:], in_=w1_hbm[:, :, f * BANK : (f + 1) * BANK])

        def load_emb(g, t0, t1):
            sync.dma_start(out=emb_rows[g][:, t0:t1, :], in_=emb_hbm[g][:, t0:t1, :])

        def load_teacher(g, c0, c1):
            cols = slice(c0 * BANK, c1 * BANK)
            sync.dma_start(out=teach_bytes[g][:, :, cols], in_=teach_hbm[g][:, :, cols])

        nc.gpsimd.memset(dummy[:], 0.0)
        scalar.dma_start(out=gain_col[:], in_=gain.rearrange("(g p t) -> p g t", p=P, t=T))
        scalar.dma_start(out=weight_col[:], in_=level_weight.rearrange("(g p t) -> p g t", p=P, t=T))
        scalar.dma_start(out=factor_col[:], in_=teacher_scale.rearrange("(g p t) o -> p g (t o)", p=P, t=T))
        scalar.activation(out=dummy[:, 0:1], in_=dummy[:, 1:2], func=ACT.Silu)
        make_identity(nc, identity[:])
        vector.memset(t_scales[:].rearrange("p g n -> p (g n)").bitcast(I32), 0)

        load_w1(0)
        load_emb(0, 0, 2)
        load_emb(0, 2, 4)
        load_w1(1)
        load_teacher(0, 0, 1)
        for g in range(GROUPS):
            sync.dma_start(out=t_words[:, g, :].bitcast(I32), in_=table_words[g].bitcast(I32))
        for q in range(4):
            sync.dma_start(
                out=t_scales[32 * q : 32 * q + 4, :, :].bitcast(I32),
                in_=table_scales[:, 4 * q : 4 * q + 4, :].rearrange("g q n -> q g n").bitcast(I32),
            )
        load_emb(1, 0, 4)
        load_teacher(1, 0, 1)
        load_teacher(0, 1, CHUNKS)
        load_teacher(1, 1, CHUNKS)

        BANKS = {"z": 2, "turned": 2, "rest": 4}

        def new_bank(tag):
            return psum.tile([P, BANK], F32, name="bank_" + tag, tag=tag, bufs=BANKS[tag])

        def new_work(tag, shape, dtype, bufs):
            return work.tile([P] + shape, dtype, name=tag, tag=tag, bufs=bufs, align_bytes=64)

        def copy(engine, out, in_):
            if engine is scalar:
                scalar.copy(out=out, in_=in_)
            else:
                vector.tensor_copy(out=out, in_=in_)

        def quantize(codes, scales, values):
            vector.quantize_mx(out=codes.bitcast(FP8X4), scales=scales, in_=values)

        def interleave(engine, out, rows):
            copy(
                engine,
                out.rearrange("p (c i) t -> p c t i", i=RUN),
                rows.rearrange("p t (c i) -> p c t i", i=RUN),
            )

        def emb_turn(g, half, tag):
            turned = new_bank(tag)
            for s in range(2):
                words = emb_rows[g][:, 2 * half + s, :].bitcast(F32)
                for u in range(2):
                    at = (2 * s + u) * P
                    tensor.transpose(turned[:, at : at + P], words[:, u : FEATURES // 2 : 2], identity[:])
            return turned

        def emb_interleave(engine, g, half, turned):
            pair = emb_mixed[g][:, 2 * half : 2 * half + 2, :, :].rearrange("p v r k -> p v (r k)")
            copy(
                engine,
                pair.bitcast(F32).rearrange("p v (r u) -> p v r u", u=2),
                turned[:].rearrange("p (v u r) -> p v r u", v=2, u=2),
            )

        def emb_quantize(g, half):
            cols = slice(2 * half * P, (2 * half + 2) * P)
            values = emb_mixed[g][:, 2 * half : 2 * half + 2, :, :].rearrange("p v r k -> p (v r k)")
            quantize(emb_codes[g][:, cols], emb_scales[g][:, cols], values)

        def w1_interleave(engine, f, n0, n1):
            interleave(engine, w1_mixed[f][:, n0:n1, :], w1_rows[f][:, :, n0:n1])

        def w1_quantize(f):
            quantize(w1_codes[f][:], w1_scales[f][:], w1_mixed[f][:].rearrange("p n t -> p (n t)"))

        z_bank = {}

        def z_matmul(i, f):
            g, t = divmod(i, T)
            z_bank[i, f] = new_bank("z")
            tensor.matmul_mx(
                out=z_bank[i, f][:],
                lhsT=emb_codes[g][:, t * P : (t + 1) * P].bitcast(FP8X4),
                lhsT_scale=emb_scales[g][:, t * P : (t + 1) * P],
                rhs=w1_codes[f][:].bitcast(FP8X4),
                rhs_scale=w1_scales[f][:],
                start=True,
                stop=True,
            )

        def silu(i, f):
            g, t = divmod(i, T)
            scalar.activation(
                out=h[g][f][:, t, :].rearrange("p (t c) -> p t c", t=T),
                in_=z_bank.pop((i, f))[:].rearrange("p (c t) -> p t c", t=T),
                func=ACT.Silu,
            )

        h_turned = {}
        a_mixed = {}
        a_quantized = {}
        bias_bank = {}
        bias_rows = {}

        def h_turn(i, f):
            g, t = divmod(i, T)
            h_turned[i, f] = new_bank("turned")
            for s in range(T):
                cols = slice(s * P, (s + 1) * P)
                tensor.transpose(h_turned[i, f][:, cols], h[g][f][:, t, cols], identity[:])

        def a_multiply(i, f):
            if i not in a_mixed:
                a_mixed[i] = new_work("a_mixed", [GROUPS, P, T], BF16, 3)
            vector.tensor_tensor(
                out=a_mixed[i][:, f, :, :],
                in0=h_turned.pop((i, f))[:].rearrange("p (t r) -> p r t", t=T),
                in1=gain_col[:, f, :].unsqueeze(1).to_broadcast([P, P, T]),
                op=MULT,
            )

        def a_quantize(i):
            codes = new_work("a_codes", [GROUPS * P], U32, 3)
            scales = new_work("a_scales", [GROUPS * P], U8, 3)
            quantize(codes[:], scales[:], a_mixed.pop(i)[:].rearrange("p f r t -> p (f r t)"))
            a_quantized[i] = (codes, scales)

        def bias_matmul(i, c):
            codes, scales = a_quantized[i]
            bias_bank[i, c] = new_bank("rest")
            for f in range(GROUPS):
                tensor.matmul_mx(
                    out=bias_bank[i, c][:],
                    lhsT=codes[:, f * P : (f + 1) * P].bitcast(FP8X4),
                    lhsT_scale=scales[:, f * P : (f + 1) * P],
                    rhs=t_words[:, f, 2 * BANK * c : 2 * BANK * (c + 1)].bitcast(FP4X4),
                    rhs_scale=t_scales[:, f, BANK * c : BANK * (c + 1)],
                    start=(f == 0),
                    stop=(f == GROUPS - 1),
                )

        def bias_out(i, c):
            g, t = divmod(i, T)
            if c == 0:
                bias_rows[i] = new_work("bias_rows", [COLS], F32, 4)
            scalar.copy(out=bias_rows[i][:, c * BANK : (c + 1) * BANK], in_=bias_bank.pop((i, c))[:])
            if c == CHUNKS - 1:
                sync.dma_start(out=bias_hbm[g, t], in_=bias_rows.pop(i)[:])

        b_mixed = {}

        def b_multiply(g, f):
            b_mixed[g, f] = new_work("b_mixed", [BANK, T], BF16, 2)
            runs = BANK // RUN_F32
            vector.tensor_tensor(
                out=b_mixed[g, f][:].rearrange("p (c i) t -> p c t i", i=RUN_F32),
                in0=h[g][f][:].rearrange("p t (c i) -> p c t i", i=RUN_F32),
                in1=weight_col[:, g, :].unsqueeze(1).unsqueeze(3).to_broadcast([P, runs, T, RUN_F32]),
                op=MULT,
            )

        def b_quantize(g, f):
            quantize(b_codes[g][f][:], b_scales[g][f][:], b_mixed.pop((g, f))[:].rearrange("p n t -> p (n t)"))

        wide = {}
        teach_mixed = {}

        def widen(engine, g, c, t):
            if (g, c) not in wide:
                wide[g, c] = new_work("wide", [T, BANK], BF16, 3)
            out = wide[g, c][:, t, :]
            values = teach_bytes[g][:, t, c * BANK : (c + 1) * BANK].bitcast(FP8)
            factor = factor_col[:, g, t : t + 1]
            if engine is scalar:
                scalar.activation(out=out, in_=values, func=ACT.Copy, scale=factor)
            else:
                vector.tensor_scalar(out=out, in0=values, scalar1=factor, scalar2=None, op0=MULT)

        def teach_interleave(g, c):
            teach_mixed[g, c] = new_work("teach_mixed", [BANK, T], BF16, 2)
            interleave(vector, teach_mixed[g, c][:], wide.pop((g, c))[:])

        def teach_quantize(g, c):
            quantize(teach_codes[g][c][:], teach_scales[g][c][:], teach_mixed.pop((g, c))[:].rearrange("p n t -> p (n t)"))

        def moments_matmul(c, j):
            f, s = divmod(j, T)
            bank = new_bank(["rest", "z", "rest", "turned"][j % 4])
            for g in range(GROUPS):
                tensor.matmul_mx(
                    out=bank[:],
                    lhsT=b_codes[g][f][:, s * P : (s + 1) * P].bitcast(FP8X4),
                    lhsT_scale=b_scales[g][f][:, s * P : (s + 1) * P],
                    rhs=teach_codes[g][c][:].bitcast(FP8X4),
                    rhs_scale=teach_scales[g][c][:],
                    start=(g == 0),
                    stop=(g == GROUPS - 1),
                )
            return bank

        def moments_out(engine, c, j, bank):
            f, s = divmod(j, T)
            rows = new_work("moment_rows", [BANK], F32, 12)
            copy(engine, rows[:], bank[:])
            sync.dma_start(out=moments_hbm[f, s][:, c * BANK : (c + 1) * BANK], in_=rows[:])


        w1_interleave(scalar, 0, 352, BANK)
        w1_interleave(vector, 0, 0, 352)
        emb_interleave(scalar, 0, 0, emb_turn(0, 0, "turned"))
        w1_quantize(0)
        emb_quantize(0, 0)
        emb_interleave(scalar, 0, 1, emb_turn(0, 1, "turned"))
        z_matmul(0, 0)
        z_matmul(1, 0)
        emb_quantize(0, 1)
        w1_interleave(scalar, 1, 0, 128)
        w1_interleave(vector, 1, 128, BANK)
        silu(0, 0)
        silu(1, 0)
        widen(vector, 0, 0, 0)
        w1_quantize(1)
        widen(scalar, 0, 0, 3)
        h_turn(0, 0)
        widen(vector, 0, 0, 1)
        widen(vector, 0, 0, 2)
        z_matmul(0, 1)
        z_matmul(1, 1)
        silu(0, 1)
        silu(1, 1)
        h_turn(1, 0)
        a_multiply(0, 0)
        teach_interleave(0, 0)
        a_multiply(1, 0)
        h_turn(0, 1)
        a_multiply(0, 1)
        for f in range(GROUPS):
            z_matmul(2, f)
            silu(2, f)
        turned = [emb_turn(1, half, "rest") for half in range(2)]
        for half in range(2):
            emb_interleave(scalar, 1, half, turned[half])
        teach_quantize(0, 0)
        a_quantize(0)
        h_turn(1, 1)
        a_multiply(1, 1)
        for f in range(GROUPS):
            z_matmul(3, f)
            silu(3, f)
        emb_quantize(1, 0)
        a_quantize(1)
        for f in range(GROUPS):
            h_turn(2, f)
            a_multiply(2, f)
        widen(scalar, 1, 0, 0)
        for f in range(GROUPS):
            z_matmul(4, f)
            silu(4, f)
        b_multiply(0, 0)

        bias_tiles = {3: [0], 4: [1, 2], 5: [3, 4], 6: [5], 7: [6, 7]}
        vector_work = {
            3: [(emb_quantize, 1, 1), (a_quantize, 2)],
            4: [(a_quantize, 3), (b_multiply, 0, 1), (a_quantize, 4), (widen, vector, 1, 0, 3), (b_quantize, 0, 0)],
            5: [(b_quantize, 0, 1), (a_quantize, 5)],
            6: [(teach_interleave, 1, 0), (a_quantize, 6), (b_multiply, 1, 0)],
            7: [(teach_quantize, 1, 0), (a_quantize, 7), (b_quantize, 1, 0), (b_multiply, 1, 1), (b_quantize, 1, 1)],
        }
        scalar_widens = {0: (1, 0, 1), 1: (1, 0, 2), 5: (1, 1, 0), 6: (0, 1, 0), 7: (0, 1, 1)}
        for k in range(3, TILES):
            if k not in (5, 6):
                for f in range(GROUPS):
                    h_turn(k, f)
            for f in range(GROUPS):
                a_multiply(k, f)
            for piece, *args in vector_work[k]:
                piece(*args)
            for i in bias_tiles[k]:
                if i in (2, 4):
                    for f in range(GROUPS):
                        h_turn(k + 1, f)
                for c in range(CHUNKS):
                    bias_matmul(i, c)
                    bias_out(i, c)
                    if i < 3 and c < GROUPS:
                        z_matmul(i + 5, c)
                        silu(i + 5, c)
                if i in scalar_widens:
                    widen(scalar, *scalar_widens[i])

        teacher_work = {
            (0, 0): [(widen, vector, 1, 1, 1), (widen, vector, 1, 1, 2), (widen, vector, 1, 1, 3), (teach_interleave, 1, 1)],
            (0, 1): [(widen, scalar, 0, 1, 2), (widen, vector, 0, 1, 3)],
            (0, 2): [(teach_quantize, 1, 1), (teach_interleave, 0, 1)],
            (0, 3): [(widen, scalar, 0, 2, 0)],
            (0, 4): [(widen, vector, 0, 2, 1), (teach_quantize, 0, 1), (widen, vector, 0, 2, 2), (widen, vector, 0, 2, 3)],
            (0, 5): [(widen, vector, 1, 2, 1), (widen, vector, 1, 2, 2)],
            (0, 6): [(teach_interleave, 0, 2)],
            (0, 7): [(widen, scalar, 1, 2, 0)],
            (1, 0): [(widen, vector, 1, 2, 3), (teach_quantize, 0, 2)],
            (1, 1): [(teach_interleave, 1, 2)],
            (1, 2): [(teach_quantize, 1, 2)],
        }
        for c in range(CHUNKS):
            for j in range(TILES):
                bank = moments_matmul(c, j)
                for piece, *args in teacher_work.get((c, j), []):
                    piece(*args)
                engine = vector if c == CHUNKS - 1 and j % 2 == 0 else scalar
                moments_out(engine, c, j, bank)
